import numpy as np, ml_dtypes
CORES = [3,5,19,21,35,37,51,53,67,69]
N = 10
import mx_ref
NC, G = 128, 4
C = np.float32(0.037)
BF = ml_dtypes.bfloat16
def tile(rs):
    return np.stack(rs, axis=2).reshape(128, -1).astype(BF)
def act(Z):
    return [np.maximum(z, 0) * C for z in Z]
def pk(c, s, i=0):
    return (np.ascontiguousarray(c[:, 512 * i:512 * i + 512]), mx_ref.live(s[:, 128 * i:128 * i + 128]))
def inputs(rng, e, E):
    def f(*shape):
        v = (rng.standard_normal(shape, dtype=np.float32) * np.exp2(rng.integers(-2, 3, shape[:-1] + (1,)))).astype(BF)
        return mx_ref.spread((v.astype(np.float32) * np.exp2(rng.integers(-E, E + 1, shape[:-2] + (1, 1))).astype(np.float32)).astype(BF), rng, e)
    def packed(k):
        c = np.zeros((N, 128, k * 512), np.uint8); s = np.zeros((N, 128, k * 128), np.uint8)
        for r in range(N):
            for i in range(k):
                a, b = mx_ref.quantize(f(128, 512)); c[r][:, 512 * i:512 * i + 512] = a; s[r][:, 128 * i:128 * i + 128] = mx_ref.plane(b, rng)
        return c, s
    d = {}
    d["ac"], d["az"] = packed(1)
    d["bc"], d["bs"] = packed(1)
    d["cc"], d["cs"] = packed(1)
    d["x"] = f(N, 128, 4 * NC)
    return d
def setup_inputs(rng):
    return inputs(rng, 0, 0)
def setup_inputs_blocks(rng):
    return inputs(rng, 2, 0)
def setup_inputs_wide(rng):
    return inputs(rng, 0, 4)
def reference(ac, az, bc, bs, cc, cs, x):
    y = np.zeros((N, 128, N * NC), np.float32)
    for r in range(N):
        h = mx_ref.quantize(tile(act([mx_ref.matmul(pk(ac[i], az[i]), mx_ref.quantize(x[r])) for i in range(G)])))
        h = mx_ref.quantize(tile(act([mx_ref.matmul(pk(bc[i], bs[i]), h) for i in range(G)])))
        for j in range(N):
            y[r][:, NC * j:NC * j + NC] = mx_ref.matmul(pk(cc[j], cs[j]), h)
    return {"y": y}

@@ -1,0 +1,274 @@
+from concourse.bass import DstId, RemoteDMATransfer
+from concourse.mybir import dt, AluOpType, ActivationFunctionType
+
+N = 10
+G = 4
+NC = 128
+SCALE = 0.037
+
+SCRATCH = {
+    "tx": ("sbuf", [128, 4 * NC], "bfloat16"),
+    "t2": ("sbuf", [128, 4 * NC], "bfloat16"),
+    "q1": ("sbuf", [128, 2 * NC], "float8_e4m3fn_x4"),
+    "q1s": ("sbuf", [128, 2 * NC], "uint8"),
+    "q2": ("sbuf", [128, 2 * NC], "float8_e4m3fn_x4"),
+    "q2s": ("sbuf", [128, 2 * NC], "uint8"),
+    "q3": ("sbuf", [128, NC], "float8_e4m3fn_x4"),
+    "q3s": ("sbuf", [128, NC], "uint8"),
+    "w": ("sbuf", [128, 2 * NC], "float8_e4m3fn_x4"),
+    "ws": ("sbuf", [128, 2 * NC], "uint8"),
+    "wc": ("sbuf", [128, 2 * NC], "float8_e4m3fn_x4"),
+    "wcs": ("sbuf", [128, 2 * NC], "uint8"),
+    "stage": ("sbuf", [128, 2 * NC], "float32"),
+    "ps": ("psum", [128, 4096], "float32"),
+}
+SEMAPHORES = ["sent", "cA", "cPA", "cB", "cPBC", "cC", "lx", "mm", "vv", "aa", "xq", "gq", "hq"]
+for _k, _n in (("a", G), ("b", G), ("c", N)):
+    for _j in range(_n):
+        SCRATCH["d%s%d" % (_k, _j)] = ("dram", [128, NC], "float8_e4m3fn_x4")
+        SCRATCH["p%s%d" % (_k, _j)] = ("dram", [128, NC], "uint8")
+        SEMAPHORES += ["d%s%d" % (_k, _j), "p%s%d" % (_k, _j)]
+SEMAPHORES += ["lw%d" % _j for _j in range(G)] + ["lc%d" % _j for _j in range(N)] + ["st%d" % _j for _j in range(N // 2)]
+
+
+def _bits(mask):
+    return [1 << i for i in range(32) if mask >> i & 1]
+
+
+def _split(bits, shares):
+    out, i = [], 0
+    for n in shares:
+        out.append(sum(bits[i:i + n]))
+        i += n
+    return out
+
+
+def _others(T, topo, r):
+    c = T.cores[r]
+    partner = [s for s in range(N) if s != r and topo.chip(T.cores[s]) == topo.chip(c)][0]
+    peers = [s for s in range(N) if topo.chip(T.cores[s]) != topo.chip(c) and topo.die(T.cores[s]) == topo.die(c)]
+    return partner, peers
+
+
+def _plan(T, topo, r):
+    partner, peers = _others(T, topo, r)
+    core = T.cores[r]
+    even = r < partner
+    off = _bits(topo.mask(core, T.cores[peers[0]]))
+    every = _bits(topo.mask(core, T.cores[partner]))
+    on = [b for b in every if b not in off]
+    offm, onm = sum(off), sum(on)
+    near = [s for s in peers if s < G]
+    far = [s for s in peers if s >= G]
+    a_users = [s for s in range(0, N, 2) if s != r and s != partner]
+    b_users = [s for s in range(1, N, 2) if s != r and s != partner]
+    wide = on if r < G else every
+    calls = []
+
+    def tile(k, mask, dsts):
+        name = "%s%d" % (k, r)
+        return (name, name, name, mask, dsts)
+
+    def send_x():
+        calls.append(([("vv", 1)], [("q3c", "q1vc", "xq", onm, [partner])]))
+        calls.append(([], [("q3s", "q1vs", "xq", onm, [partner])]))
+
+    if r < G:
+        calls.append(([("cA", 16)], [tile("da", offm, a_users)]))
+        calls.append(([("cPA", 16)], [tile("pa", offm, a_users)]))
+        if not even:
+            send_x()
+        calls.append(([("cB", 16)], [tile("db", offm, b_users), tile("db" if even else "da", onm, [partner])]))
+        h, m = _split(off, (4, 4)), _split(on, (4, 4))
+        calls.append(([("cPBC", 32)], [tile("pb", h[0], b_users), tile("pc", h[1], peers),
+                                       tile("pb" if even else "pa", m[0], [partner]), tile("pc", m[1], [partner])]))
+        calls.append(([("cC", 16)], [tile("dc", offm, peers), tile("dc", onm, [partner])]))
+    else:
+        if not even:
+            send_x()
+        calls.append(([("cC", 16)], [tile("dc", offm, peers), tile("dc", onm, [partner])]))
+        calls.append(([("cPBC", 16)], [tile("pc", offm, peers), tile("pc", onm, [partner])]))
+
+    def forward(names):
+        n = len(wide)
+        sizes = {1: (n,), 2: (n // 2,) * 2, 3: (n // 2, n // 4, n // 4)}[len(names)]
+        calls.append(([(x, None) for x in names],
+                      [(x, x, x, mk, [partner]) for x, mk in zip(names, _split(wide, sizes))]))
+
+    forward(["dc%d" % s for s in far])
+    forward(["pc%d" % s for s in far])
+    wm = sum(wide)
+    if even:
+        calls.append(([("vv", 7)], [("q2c", "q1c", "gq", wm, [partner])]))
+        calls.append(([], [("q2s", "q1s", "gq", wm, [partner])]))
+    else:
+        calls.append(([("vv", 4)], [("q2uc", "q3c", "hq", wm, [partner])]))
+        calls.append(([], [("q2us", "q3s", "hq", wm, [partner])]))
+    forward(["dc%d" % s for s in near])
+    forward(["pc%d" % s for s in near])
+    return calls
+
+
+def rank_program(g, core, T, topo):
+    r = T.rank_of(core)
+    if r is None:
+        return
+    partner, peers = _others(T, topo, r)
+    even = r < partner
+    holds = r < G
+    lk = "a" if even else "b"
+
+    arrive = {}
+    for s in range(N):
+        if s != r:
+            for _, transfers in _plan(T, topo, s):
+                for _, _, sem, mask, dsts in transfers:
+                    if r in dsts:
+                        arrive[sem] = arrive.get(sem, 0) + len(_bits(mask))
+
+    views = {"q1c": T.q1[:].bitcast(dt.uint8), "q1s": T.q1s[:],
+             "q1vc": T.q1[:, NC:2 * NC].bitcast(dt.uint8), "q1vs": T.q1s[:, NC:2 * NC],
+             "q2c": T.q2[:].bitcast(dt.uint8), "q2s": T.q2s[:],
+             "q2uc": T.q2[:, 0:NC].bitcast(dt.uint8), "q2us": T.q2s[:, 0:NC],
+             "q3c": T.q3[:].bitcast(dt.uint8), "q3s": T.q3s[:]}
+
+    def raw(name):
+        if name in views:
+            return views[name]
+        return T[name][:].bitcast(dt.uint8) if name[0] == "d" else T[name][:]
+
+    own = {"da": T.ac, "pa": T.az, "db": T.bc, "pb": T.bs, "dc": T.cc, "pc": T.cs}
+
+    copies = [("da", "cA"), ("pa", "cPA"), ("db", "cB"), ("pb", "cPBC"), ("pc", "cPBC"), ("dc", "cC")] if holds else \
+             [("dc", "cC"), ("pc", "cPBC")]
+    for k, sem in copies:
+        g.scalar.dma_start(raw("%s%d" % (k, r)), own[k][:]).then_inc(T.sem[sem], 16)
+
+    sent = 0
+    for waits, transfers in _plan(T, topo, r):
+        for sem, count in waits:
+            g.wait_ge(T.sem[sem], arrive[sem] if count is None else count)
+        out = []
+        for src, dst, sem, mask, dsts in transfers:
+            ids = []
+            for d in dsts:
+                rid, pid, _ = topo.addr(T.cores[d])
+                ids.append(DstId(rid=rid, pnc=pid))
+            out.append(RemoteDMATransfer(dst_ids=ids, dma_engine_mask=mask, remote_sem=T.sem[sem],
+                                         srcs=[raw(src)], dsts=[raw(dst) for _ in dsts]))
+            sent += len(_bits(mask))
+        g.remote_dma_fused(out, local_sem=T.sem.sent)
+    g.wait_ge(T.sem.sent, sent)
+
+    pairs = sorted(range(N // 2), key=lambda p: (r // 2 != p, 2 * p < G, p))
+    cs = [s for p in pairs for s in (2 * p, 2 * p + 1)]
+    ws = sorted(range(G), key=lambda s: (s != r, s != partner, s))
+    order = {"w": ws, "c": cs}
+    kind = {"w": lk, "c": "c"}
+    slots = {"w": (T.w, T.ws), "c": (T.wc, T.wcs)}
+    first = {"w": 0, "c": G}
+
+    def slot(k, i):
+        a = (i % 2) * NC
+        return slots[k][0][:, a:a + NC], slots[k][1][:, a:a + NC]
+
+    def load(k, i):
+        s = order[k][i]
+        w, wp = slot(k, i)
+        if i >= 2:
+            g.sync.wait_ge(T.sem.mm, first[k] + i - 1)
+        sem = T.sem["l%s%d" % (k, i)]
+        for c, view in (("d", w.bitcast(dt.uint8)), ("p", wp)):
+            name = "%s%s%d" % (c, kind[k], s)
+            if s == r:
+                g.sync.dma_start(view, own[c + kind[k]][:]).then_inc(sem, 16)
+            else:
+                g.sync.wait_ge(T.sem[name], arrive[name])
+                g.sync.dma_start(view, raw(name)).then_inc(sem, 16)
+
+    g.sync.dma_start(T.tx[:], T.x[:]).then_inc(T.sem.lx, 16)
+    mine = cs.index(r)
+    seq = ([("w", 0)] if holds else []) + [("c", mine)]
+    rest = ([] if holds else [("w", 0)]) + [("w", 1)]
+    if even:
+        seq += rest + [("w", 2), ("w", 3), ("c", 1 - mine)]
+    else:
+        seq += rest + [("c", 1 - mine), ("w", 2), ("w", 3)]
+    seq += [("c", i) for i in range(2, N)]
+    for k, i in seq:
+        load(k, i)
+
+    def bank(n):
+        return (n % 8) * 512
+
+    if even:
+        g.tensor.wait_ge(T.sem.vv, 1)
+        g.tensor.wait_ge(T.sem.xq, arrive["xq"])
+    else:
+        g.tensor.wait_ge(T.sem.gq, arrive["gq"])
+    for i in range(G):
+        g.tensor.wait_ge(T.sem["lw%d" % i], 32)
+        w, wp = slot("w", i)
+        g.tensor.matmul_mx(T.ps[:, bank(i):bank(i) + 2 * NC], w, wp, T.q1[:], T.q1s[:], True, True).then_inc(T.sem.mm, 1)
+    if even:
+        g.tensor.wait_ge(T.sem.hq, arrive["hq"])
+        hq, hs = T.q3[:], T.q3s[:]
+    else:
+        g.tensor.wait_ge(T.sem.vv, 7)
+        hq, hs = T.q2[:, NC:2 * NC], T.q2s[:, NC:2 * NC]
+    g.tensor.wait_ge(T.sem.aa, 4)
+    g.tensor.wait_ge(T.sem.vv, 7)
+    for i in range(N):
+        n = G + i
+        if i == 8:
+            g.tensor.wait_ge(T.sem.vv, 8)
+        if i == 9:
+            g.tensor.wait_ge(T.sem.aa, 5)
+        g.tensor.wait_ge(T.sem["lc%d" % i], 32)
+        w, wp = slot("c", i)
+        g.tensor.matmul_mx(T.ps[:, bank(n):bank(n) + NC], w, wp, hq, hs, True, True).then_inc(T.sem.mm, 1)
+
+    g.vector.wait_ge(T.sem.lx, 16)
+    if even:
+        g.vector.quantize_mx(T.q1[:, 0:NC], T.q1s[:, 0:NC], T.tx[:]).then_inc(T.sem.vv, 1)
+    else:
+        g.vector.quantize_mx(T.q3[:], T.q3s[:], T.tx[:]).then_inc(T.sem.vv, 1)
+    for half in range(2):
+        a = half * NC
+        if half:
+            g.vector.wait_ge(T.sem.vv, 4)
+        for i in (0, 2):
+            b = ws[i]
+            g.vector.wait_ge(T.sem.mm, i + 1)
+            g.vector.tensor_scalar(T.t2[:, b:4 * NC:4], T.ps[:, bank(i) + a:bank(i) + a + NC], 0.0, SCALE,
+                                   AluOpType.max, AluOpType.mult).then_inc(T.sem.vv, 1)
+        g.vector.wait_ge(T.sem.vv, 3 + 3 * half)
+        g.vector.wait_ge(T.sem.aa, 2 + 2 * half)
+        g.vector.quantize_mx(T.q2[:, a:a + NC], T.q2s[:, a:a + NC], T.t2[:]).then_inc(T.sem.vv, 1)
+    for p in range(N // 2):
+        n = G + 2 * p
+        if p >= 1:
+            g.vector.wait_ge(T.sem["st%d" % (p - 1)], 16)
+        g.vector.wait_ge(T.sem.mm, n + 1)
+        g.vector.tensor_copy(T.stage[:, 0:NC], T.ps[:, bank(n):bank(n) + NC]).then_inc(T.sem.vv, 1)
+
+    for half in range(2):
+        a = half * NC
+        if half:
+            g.scalar.wait_ge(T.sem.vv, 4)
+        for i in (1, 3):
+            b = ws[i]
+            g.scalar.wait_ge(T.sem.mm, i + 1)
+            g.scalar.activation(T.t2[:, b:4 * NC:4], T.ps[:, bank(i) + a:bank(i) + a + NC],
+                                ActivationFunctionType.Relu, scale=SCALE).then_inc(T.sem.aa, 1)
+    for p in range(N // 2):
+        n = G + 2 * p + 1
+        if p >= 1:
+            g.scalar.wait_ge(T.sem["st%d" % (p - 1)], 16)
+        g.scalar.wait_ge(T.sem.mm, n + 1)
+        g.scalar.activation(T.stage[:, NC:2 * NC], T.ps[:, bank(n):bank(n) + NC], ActivationFunctionType.Copy).then_inc(T.sem.aa, 1)
+        g.scalar.wait_ge(T.sem.vv, 8 + p)
+        g.scalar.wait_ge(T.sem.aa, 5 + p)
+        y = pairs[p] * 2 * NC
+        g.scalar.dma_start(T.y[:, y:y + 2 * NC], T.stage[:]).then_inc(T.sem["st%d" % p], 16)
+    g.scalar.wait_ge(T.sem["st%d" % (N // 2 - 1)], 16)

@@ -2,237 +2,275 @@ from concourse.bass import DstId, RemoteDMATransfer
 from concourse.mybir import dt, AluOpType, ActivationFunctionType
 
 N = 10
+P = N // 2
 G = 4
 NC = 128
+SIM = 80
 SCALE = 0.037
 
+CODES, PLANE = "float8_e4m3fn_x4", "uint8"
 SCRATCH = {
     "tx": ("sbuf", [128, 4 * NC], "bfloat16"),
     "t2": ("sbuf", [128, 4 * NC], "bfloat16"),
-    "q1": ("sbuf", [128, 2 * NC], "float8_e4m3fn_x4"),
-    "q1s": ("sbuf", [128, 2 * NC], "uint8"),
-    "q2": ("sbuf", [128, 2 * NC], "float8_e4m3fn_x4"),
-    "q2s": ("sbuf", [128, 2 * NC], "uint8"),
-    "q3": ("sbuf", [128, NC], "float8_e4m3fn_x4"),
-    "q3s": ("sbuf", [128, NC], "uint8"),
-    "w": ("sbuf", [128, 2 * NC], "float8_e4m3fn_x4"),
-    "ws": ("sbuf", [128, 2 * NC], "uint8"),
-    "wc": ("sbuf", [128, 2 * NC], "float8_e4m3fn_x4"),
-    "wcs": ("sbuf", [128, 2 * NC], "uint8"),
+    "q1": ("sbuf", [128, 2 * NC], CODES),
+    "q1s": ("sbuf", [128, 2 * NC], PLANE),
+    "q2": ("sbuf", [128, 2 * NC], CODES),
+    "q2s": ("sbuf", [128, 2 * NC], PLANE),
+    "q3": ("sbuf", [128, NC], CODES),
+    "q3s": ("sbuf", [128, NC], PLANE),
+    "w": ("sbuf", [128, 2 * NC], CODES),
+    "ws": ("sbuf", [128, 2 * NC], PLANE),
+    "wc": ("sbuf", [128, 2 * NC], CODES),
+    "wcs": ("sbuf", [128, 2 * NC], PLANE),
     "stage": ("sbuf", [128, 2 * NC], "float32"),
     "ps": ("psum", [128, 4096], "float32"),
+    "sc": ("dram", [128, NC], CODES),
+    "sp": ("dram", [128, NC], PLANE),
 }
-SEMAPHORES = ["sent", "cA", "cPA", "cB", "cPBC", "cC", "lx", "mm", "vv", "aa", "xq", "gq", "hq"]
-for _k, _n in (("a", G), ("b", G), ("c", N)):
-    for _j in range(_n):
-        SCRATCH["d%s%d" % (_k, _j)] = ("dram", [128, NC], "float8_e4m3fn_x4")
-        SCRATCH["p%s%d" % (_k, _j)] = ("dram", [128, NC], "uint8")
+SEMAPHORES = ["sent", "cA", "cPA", "cB", "cPB", "cC", "cPC", "lx", "mm", "vv", "aa", "xq", "gq", "hq", "hl"]
+for _j in range(G):
+    for _k in ("a", "b"):
+        SCRATCH["d%s%d" % (_k, _j)] = ("dram", [128, NC], CODES)
+        SCRATCH["p%s%d" % (_k, _j)] = ("dram", [128, NC], PLANE)
         SEMAPHORES += ["d%s%d" % (_k, _j), "p%s%d" % (_k, _j)]
-SEMAPHORES += ["lw%d" % _j for _j in range(G)] + ["lc%d" % _j for _j in range(N)] + ["st%d" % _j for _j in range(N // 2)]
+    SEMAPHORES += ["lw%d" % _j]
+for _j in range(2):
+    SCRATCH["dh%d" % _j] = ("dram", [128, NC], CODES)
+    SCRATCH["ph%d" % _j] = ("dram", [128, NC], PLANE)
+    SEMAPHORES += ["dh%d" % _j, "ph%d" % _j]
+for _j in range(P):
+    SCRATCH["dc%d" % _j] = ("dram", [128, 2 * NC], CODES)
+    SCRATCH["pc%d" % _j] = ("dram", [128, 2 * NC], PLANE)
+    SEMAPHORES += ["dc%d" % _j, "pc%d" % _j, "lc%d" % _j, "st%d" % _j]
 
 
 def _bits(mask):
     return [1 << i for i in range(32) if mask >> i & 1]
 
 
-def _split(bits, shares):
-    out, i = [], 0
-    for n in shares:
-        out.append(sum(bits[i:i + n]))
-        i += n
+def _helpers(T, topo):
+    out = {}
+    for p in range(P):
+        u = T.cores[2 * p]
+        for d in (topo.die(u), topo.die(T.cores[2 * p + 1])):
+            free = [c for c in range(SIM) if topo.chip(c) == topo.chip(u) and topo.die(c) == d and T.rank_of(c) is None]
+            out[free[0]] = (p, d)
     return out
 
 
-def _others(T, topo, r):
-    c = T.cores[r]
-    partner = [s for s in range(N) if s != r and topo.chip(T.cores[s]) == topo.chip(c)][0]
-    peers = [s for s in range(N) if topo.chip(T.cores[s]) != topo.chip(c) and topo.die(T.cores[s]) == topo.die(c)]
-    return partner, peers
+def _waves(p):
+    held = G // 2
+    rest = list(range(held, P))
+    if p == 0:
+        return [1, rest[0]] + rest[1:]
+    return rest[1:] + [rest[0], 0]
 
 
-def _plan(T, topo, r):
-    partner, peers = _others(T, topo, r)
-    core = T.cores[r]
-    even = r < partner
-    off = _bits(topo.mask(core, T.cores[peers[0]]))
-    every = _bits(topo.mask(core, T.cores[partner]))
-    on = [b for b in every if b not in off]
-    offm, onm = sum(off), sum(on)
-    near = [s for s in peers if s < G]
-    far = [s for s in peers if s >= G]
-    a_users = [s for s in range(0, N, 2) if s != r and s != partner]
-    b_users = [s for s in range(1, N, 2) if s != r and s != partner]
-    wide = on if r < G else every
+def _plan(T, topo, core):
+    helpers = _helpers(T, topo)
     calls = []
+    if core in helpers:
+        p, d = helpers[core]
+        same = {helpers[h][0]: h for h in helpers if helpers[h][1] == d}
+        steps = (1, 2) if d == topo.die(T.cores[0]) else (3, 4)
+        away = [same[(p + k) % P] for k in steps]
+        ranks = [T.cores[2 * p], T.cores[2 * p + 1]]
+        here = [c for c in ranks if topo.die(c) == d]
+        off = topo.mask(core, away[0])
+        every = topo.mask(core, here[0])
+        for k in "dp":
+            name = "%sc%d" % (k, p)
+            calls.append(([("hl", 64)] if k == "d" else [],
+                          [(name, name, name, off, away), (name, name, name, every & ~off, here)]))
+        for q in sorted(((p - k) % P for k in steps), key=lambda q: (2 * q < G, q)):
+            for k in "dp":
+                name = "%sc%d" % (k, q)
+                calls.append(([(name, None)], [(name, name, name, every, ranks)]))
+        return calls
+    r = T.rank_of(core)
+    if r is None:
+        return calls
+    p, odd = divmod(r, 2)
+    partner = T.cores[r ^ 1]
+    mine = [h for h in helpers if helpers[h][0] == p]
+    a_users = [T.cores[2 * s] for s in range(P) if s != p]
+    b_users = [T.cores[2 * s + 1] for s in range(P) if s != p]
+    off = topo.mask(core, a_users[0])
+    every = topo.mask(core, partner)
+    on = every & ~off
+    b = _bits(on)
+    on1, on2 = sum(b[:len(b) // 2]), sum(b[len(b) // 2:])
 
     def tile(k, mask, dsts):
         name = "%s%d" % (k, r)
         return (name, name, name, mask, dsts)
 
-    def send_x():
-        calls.append(([("vv", 1)], [("q3c", "q1vc", "xq", onm, [partner])]))
-        calls.append(([], [("q3s", "q1vs", "xq", onm, [partner])]))
+    def send_x(mask):
+        calls.append(([("vv", 1)], [("q3c", "q1vc", "xq", mask, [partner])]))
+        calls.append(([], [("q3s", "q1vs", "xq", mask, [partner])]))
 
     if r < G:
-        calls.append(([("cA", 16)], [tile("da", offm, a_users)]))
-        calls.append(([("cPA", 16)], [tile("pa", offm, a_users)]))
-        if not even:
-            send_x()
-        calls.append(([("cB", 16)], [tile("db", offm, b_users), tile("db" if even else "da", onm, [partner])]))
-        h, m = _split(off, (4, 4)), _split(on, (4, 4))
-        calls.append(([("cPBC", 32)], [tile("pb", h[0], b_users), tile("pc", h[1], peers),
-                                       tile("pb" if even else "pa", m[0], [partner]), tile("pc", m[1], [partner])]))
-        calls.append(([("cC", 16)], [tile("dc", offm, peers), tile("dc", onm, [partner])]))
+        order = _waves(p)
+        for w in (order[:2], order[2:]):
+            dsts = [T.cores[2 * s] for s in w]
+            calls.append(([("cA", 16)], [tile("da", off, dsts)]))
+            calls.append(([("cPA", 16)], [tile("pa", off, dsts)]))
+        if odd:
+            send_x(on)
+        calls.append(([("cB", 16), ("cC", 16)], [tile("db", off, b_users), tile("da" if odd else "db", on1, [partner]),
+                                                 ("sc", "dh%d" % odd, "dh%d" % odd, on2, mine)]))
+        calls.append(([("cPB", 16), ("cPC", 16)], [tile("pb", off, b_users), tile("pa" if odd else "pb", on1, [partner]),
+                                                   ("sp", "ph%d" % odd, "ph%d" % odd, on2, mine)]))
     else:
-        if not even:
-            send_x()
-        calls.append(([("cC", 16)], [tile("dc", offm, peers), tile("dc", onm, [partner])]))
-        calls.append(([("cPBC", 16)], [tile("pc", offm, peers), tile("pc", onm, [partner])]))
-
-    def forward(names):
-        n = len(wide)
-        sizes = {1: (n,), 2: (n // 2,) * 2, 3: (n // 2, n // 4, n // 4)}[len(names)]
-        calls.append(([(x, None) for x in names],
-                      [(x, x, x, mk, [partner]) for x, mk in zip(names, _split(wide, sizes))]))
-
-    forward(["dc%d" % s for s in far])
-    forward(["pc%d" % s for s in far])
-    wm = sum(wide)
-    if even:
-        calls.append(([("vv", 7)], [("q2c", "q1c", "gq", wm, [partner])]))
-        calls.append(([], [("q2s", "q1s", "gq", wm, [partner])]))
+        if odd:
+            send_x(every)
+        calls.append(([("cC", 16)], [("sc", "dh%d" % odd, "dh%d" % odd, every, mine)]))
+        calls.append(([("cPC", 16)], [("sp", "ph%d" % odd, "ph%d" % odd, every, mine)]))
+    if odd:
+        calls.append(([("vv", 4)], [("q2uc", "q3c", "hq", every, [partner])]))
+        calls.append(([], [("q2us", "q3s", "hq", every, [partner])]))
     else:
-        calls.append(([("vv", 4)], [("q2uc", "q3c", "hq", wm, [partner])]))
-        calls.append(([], [("q2us", "q3s", "hq", wm, [partner])]))
-    forward(["dc%d" % s for s in near])
-    forward(["pc%d" % s for s in near])
+        calls.append(([("vv", 7)], [("q2c", "q1c", "gq", every, [partner])]))
+        calls.append(([], [("q2s", "q1s", "gq", every, [partner])]))
     return calls
 
 
 def rank_program(g, core, T, topo):
+    helpers = _helpers(T, topo)
     r = T.rank_of(core)
-    if r is None:
+    if r is None and core not in helpers:
         return
-    partner, peers = _others(T, topo, r)
-    even = r < partner
-    holds = r < G
-    lk = "a" if even else "b"
 
     arrive = {}
-    for s in range(N):
-        if s != r:
-            for _, transfers in _plan(T, topo, s):
+    for c in list(T.cores) + list(helpers):
+        if c != core:
+            for _, transfers in _plan(T, topo, c):
                 for _, _, sem, mask, dsts in transfers:
-                    if r in dsts:
+                    if core in dsts:
                         arrive[sem] = arrive.get(sem, 0) + len(_bits(mask))
 
     views = {"q1c": T.q1[:].bitcast(dt.uint8), "q1s": T.q1s[:],
              "q1vc": T.q1[:, NC:2 * NC].bitcast(dt.uint8), "q1vs": T.q1s[:, NC:2 * NC],
              "q2c": T.q2[:].bitcast(dt.uint8), "q2s": T.q2s[:],
              "q2uc": T.q2[:, 0:NC].bitcast(dt.uint8), "q2us": T.q2s[:, 0:NC],
-             "q3c": T.q3[:].bitcast(dt.uint8), "q3s": T.q3s[:]}
+             "q3c": T.q3[:].bitcast(dt.uint8), "q3s": T.q3s[:],
+             "sc": T.sc[:].bitcast(dt.uint8), "sp": T.sp[:]}
 
     def raw(name):
         if name in views:
             return views[name]
         return T[name][:].bitcast(dt.uint8) if name[0] == "d" else T[name][:]
 
-    own = {"da": T.ac, "pa": T.az, "db": T.bc, "pb": T.bs, "dc": T.cc, "pc": T.cs}
+    def remote():
+        sent = 0
+        for waits, transfers in _plan(T, topo, core):
+            for sem, count in waits:
+                g.wait_ge(T.sem[sem], arrive[sem] if count is None else count)
+            out = []
+            for src, dst, sem, mask, dsts in transfers:
+                ids = []
+                for d in dsts:
+                    rid, pid, _ = topo.addr(d)
+                    ids.append(DstId(rid=rid, pnc=pid))
+                out.append(RemoteDMATransfer(dst_ids=ids, dma_engine_mask=mask, remote_sem=T.sem[sem],
+                                             srcs=[raw(src)], dsts=[raw(dst) for _ in dsts]))
+                sent += len(_bits(mask))
+            g.remote_dma_fused(out, local_sem=T.sem.sent)
+        g.wait_ge(T.sem.sent, sent)
 
-    copies = [("da", "cA"), ("pa", "cPA"), ("db", "cB"), ("pb", "cPBC"), ("pc", "cPBC"), ("dc", "cC")] if holds else \
-             [("dc", "cC"), ("pc", "cPBC")]
-    for k, sem in copies:
-        g.scalar.dma_start(raw("%s%d" % (k, r)), own[k][:]).then_inc(T.sem[sem], 16)
+    if r is None:
+        p = helpers[core][0]
+        for k in "dp":
+            for j in range(2):
+                name = "%sh%d" % (k, j)
+                half = T["%sc%d" % (k, p)][:, j * NC:(j + 1) * NC]
+                g.sync.wait_ge(T.sem[name], arrive[name])
+                g.sync.dma_start(half.bitcast(dt.uint8) if k == "d" else half, raw(name)).then_inc(T.sem.hl, 16)
+        remote()
+        return
 
-    sent = 0
-    for waits, transfers in _plan(T, topo, r):
-        for sem, count in waits:
-            g.wait_ge(T.sem[sem], arrive[sem] if count is None else count)
-        out = []
-        for src, dst, sem, mask, dsts in transfers:
-            ids = []
-            for d in dsts:
-                rid, pid, _ = topo.addr(T.cores[d])
-                ids.append(DstId(rid=rid, pnc=pid))
-            out.append(RemoteDMATransfer(dst_ids=ids, dma_engine_mask=mask, remote_sem=T.sem[sem],
-                                         srcs=[raw(src)], dsts=[raw(dst) for _ in dsts]))
-            sent += len(_bits(mask))
-        g.remote_dma_fused(out, local_sem=T.sem.sent)
-    g.wait_ge(T.sem.sent, sent)
+    pair, odd = divmod(r, 2)
+    holds = r < G
+    lk = "b" if odd else "a"
+    own = {"da": T.ac, "pa": T.az, "db": T.bc, "pb": T.bs}
 
-    pairs = sorted(range(N // 2), key=lambda p: (r // 2 != p, 2 * p < G, p))
-    cs = [s for p in pairs for s in (2 * p, 2 * p + 1)]
-    ws = sorted(range(G), key=lambda s: (s != r, s != partner, s))
-    order = {"w": ws, "c": cs}
-    kind = {"w": lk, "c": "c"}
-    slots = {"w": (T.w, T.ws), "c": (T.wc, T.wcs)}
-    first = {"w": 0, "c": G}
+    if holds:
+        for k, sem in (("da", "cA"), ("pa", "cPA"), ("db", "cB"), ("pb", "cPB")):
+            g.scalar.dma_start(raw("%s%d" % (k, r)), own[k][:]).then_inc(T.sem[sem], 16)
+    g.scalar.dma_start(raw("sc"), T.cc[:]).then_inc(T.sem.cC, 16)
+    g.scalar.dma_start(raw("sp"), T.cs[:]).then_inc(T.sem.cPC, 16)
 
-    def slot(k, i):
+    remote()
+
+    pairs = sorted(range(P), key=lambda p: (pair != p, 2 * p < G, p))
+    early = {s: pair in _waves(s)[:2] for s in range(G // 2) if s != pair}
+    ws = sorted(range(G), key=lambda s: (s != r, s // 2 != pair, not early.get(s // 2, False), s))
+
+    def slot(i):
         a = (i % 2) * NC
-        return slots[k][0][:, a:a + NC], slots[k][1][:, a:a + NC]
+        return T.w[:, a:a + NC], T.ws[:, a:a + NC]
 
-    def load(k, i):
-        s = order[k][i]
-        w, wp = slot(k, i)
+    def load(i):
+        s = ws[i]
+        w, wp = slot(i)
         if i >= 2:
-            g.sync.wait_ge(T.sem.mm, first[k] + i - 1)
-        sem = T.sem["l%s%d" % (k, i)]
+            g.sync.wait_ge(T.sem.mm, i - 1)
+        sem = T.sem["lw%d" % i]
         for c, view in (("d", w.bitcast(dt.uint8)), ("p", wp)):
-            name = "%s%s%d" % (c, kind[k], s)
+            name = "%s%s%d" % (c, lk, s)
             if s == r:
-                g.sync.dma_start(view, own[c + kind[k]][:]).then_inc(sem, 16)
+                g.sync.dma_start(view, own[c + lk][:]).then_inc(sem, 16)
             else:
                 g.sync.wait_ge(T.sem[name], arrive[name])
                 g.sync.dma_start(view, raw(name)).then_inc(sem, 16)
 
     g.sync.dma_start(T.tx[:], T.x[:]).then_inc(T.sem.lx, 16)
-    mine = cs.index(r)
-    seq = ([("w", 0)] if holds else []) + [("c", mine)]
-    rest = ([] if holds else [("w", 0)]) + [("w", 1)]
-    if even:
-        seq += rest + [("w", 2), ("w", 3), ("c", 1 - mine)]
-    else:
-        seq += rest + [("c", 1 - mine), ("w", 2), ("w", 3)]
-    seq += [("c", i) for i in range(2, N)]
-    for k, i in seq:
-        load(k, i)
+    for i in range(G):
+        load(i)
+    for i in range(P):
+        if i:
+            g.sync.wait_ge(T.sem.mm, G + 2 * i)
+        for c, view in (("d", T.wc[:].bitcast(dt.uint8)), ("p", T.wcs[:])):
+            name = "%sc%d" % (c, pairs[i])
+            g.sync.wait_ge(T.sem[name], arrive[name])
+            g.sync.dma_start(view, raw(name)).then_inc(T.sem["lc%d" % i], 16)
 
     def bank(n):
         return (n % 8) * 512
 
-    if even:
+    if odd:
+        g.tensor.wait_ge(T.sem.gq, arrive["gq"])
+    else:
         g.tensor.wait_ge(T.sem.vv, 1)
         g.tensor.wait_ge(T.sem.xq, arrive["xq"])
-    else:
-        g.tensor.wait_ge(T.sem.gq, arrive["gq"])
     for i in range(G):
         g.tensor.wait_ge(T.sem["lw%d" % i], 32)
-        w, wp = slot("w", i)
+        w, wp = slot(i)
         g.tensor.matmul_mx(T.ps[:, bank(i):bank(i) + 2 * NC], w, wp, T.q1[:], T.q1s[:], True, True).then_inc(T.sem.mm, 1)
-    if even:
-        g.tensor.wait_ge(T.sem.hq, arrive["hq"])
-        hq, hs = T.q3[:], T.q3s[:]
-    else:
-        g.tensor.wait_ge(T.sem.vv, 7)
-        hq, hs = T.q2[:, NC:2 * NC], T.q2s[:, NC:2 * NC]
     g.tensor.wait_ge(T.sem.aa, 4)
     g.tensor.wait_ge(T.sem.vv, 7)
+    if odd:
+        hq, hs = T.q2[:, NC:2 * NC], T.q2s[:, NC:2 * NC]
+    else:
+        g.tensor.wait_ge(T.sem.hq, arrive["hq"])
+        hq, hs = T.q3[:], T.q3s[:]
     for i in range(N):
         n = G + i
         if i == 8:
             g.tensor.wait_ge(T.sem.vv, 8)
         if i == 9:
             g.tensor.wait_ge(T.sem.aa, 5)
-        g.tensor.wait_ge(T.sem["lc%d" % i], 32)
-        w, wp = slot("c", i)
-        g.tensor.matmul_mx(T.ps[:, bank(n):bank(n) + NC], w, wp, hq, hs, True, True).then_inc(T.sem.mm, 1)
+        if i % 2 == 0:
+            g.tensor.wait_ge(T.sem["lc%d" % (i // 2)], 32)
+        a = (i % 2) * NC
+        g.tensor.matmul_mx(T.ps[:, bank(n):bank(n) + NC], T.wc[:, a:a + NC], T.wcs[:, a:a + NC], hq, hs,
+                           True, True).then_inc(T.sem.mm, 1)
 
     g.vector.wait_ge(T.sem.lx, 16)
-    if even:
-        g.vector.quantize_mx(T.q1[:, 0:NC], T.q1s[:, 0:NC], T.tx[:]).then_inc(T.sem.vv, 1)
-    else:
+    if odd:
         g.vector.quantize_mx(T.q3[:], T.q3s[:], T.tx[:]).then_inc(T.sem.vv, 1)
+    else:
+        g.vector.quantize_mx(T.q1[:, 0:NC], T.q1s[:, 0:NC], T.tx[:]).then_inc(T.sem.vv, 1)
     for half in range(2):
         a = half * NC
         if half:
@@ -245,7 +283,7 @@ def rank_program(g, core, T, topo):
         g.vector.wait_ge(T.sem.vv, 3 + 3 * half)
         g.vector.wait_ge(T.sem.aa, 2 + 2 * half)
         g.vector.quantize_mx(T.q2[:, a:a + NC], T.q2s[:, a:a + NC], T.t2[:]).then_inc(T.sem.vv, 1)
-    for p in range(N // 2):
+    for p in range(P):
         n = G + 2 * p
         if p >= 1:
             g.vector.wait_ge(T.sem["st%d" % (p - 1)], 16)
@@ -261,7 +299,7 @@ def rank_program(g, core, T, topo):
             g.scalar.wait_ge(T.sem.mm, i + 1)
             g.scalar.activation(T.t2[:, b:4 * NC:4], T.ps[:, bank(i) + a:bank(i) + a + NC],
                                 ActivationFunctionType.Relu, scale=SCALE).then_inc(T.sem.aa, 1)
-    for p in range(N // 2):
+    for p in range(P):
         n = G + 2 * p + 1
         if p >= 1:
             g.scalar.wait_ge(T.sem["st%d" % (p - 1)], 16)
@@ -271,4 +309,4 @@ def rank_program(g, core, T, topo):
         g.scalar.wait_ge(T.sem.aa, 5 + p)
         y = pairs[p] * 2 * NC
         g.scalar.dma_start(T.y[:, y:y + 2 * NC], T.stage[:]).then_inc(T.sem["st%d" % p], 16)
-    g.scalar.wait_ge(T.sem["st%d" % (N // 2 - 1)], 16)
+    g.scalar.wait_ge(T.sem["st%d" % (P - 1)], 16)

@@ -7,304 +7,250 @@ G = 4
 NC = 128
 SIM = 80
 SCALE = 0.037
+WA, WC = 2, 3
 
 CODES, PLANE = "float8_e4m3fn_x4", "uint8"
 SCRATCH = {
     "tx": ("sbuf", [128, 4 * NC], "bfloat16"),
     "t2": ("sbuf", [128, 4 * NC], "bfloat16"),
-    "q1": ("sbuf", [128, 2 * NC], CODES),
-    "q1s": ("sbuf", [128, 2 * NC], PLANE),
-    "q2": ("sbuf", [128, 2 * NC], CODES),
-    "q2s": ("sbuf", [128, 2 * NC], PLANE),
-    "q3": ("sbuf", [128, NC], CODES),
-    "q3s": ("sbuf", [128, NC], PLANE),
-    "w": ("sbuf", [128, 2 * NC], CODES),
-    "ws": ("sbuf", [128, 2 * NC], PLANE),
-    "wc": ("sbuf", [128, 2 * NC], CODES),
-    "wcs": ("sbuf", [128, 2 * NC], PLANE),
+    "qx": ("sbuf", [128, NC], CODES),
+    "qxs": ("sbuf", [128, NC], PLANE),
+    "q2": ("sbuf", [128, NC], CODES),
+    "q2s": ("sbuf", [128, NC], PLANE),
+    "wa": ("sbuf", [128, WA * NC], CODES),
+    "was": ("sbuf", [128, WA * NC], PLANE),
+    "wb": ("sbuf", [128, WA * NC], CODES),
+    "wbs": ("sbuf", [128, WA * NC], PLANE),
+    "wc": ("sbuf", [128, WC * NC], CODES),
+    "wcs": ("sbuf", [128, WC * NC], PLANE),
     "stage": ("sbuf", [128, 2 * NC], "float32"),
     "ps": ("psum", [128, 4096], "float32"),
-    "sc": ("dram", [128, NC], CODES),
-    "sp": ("dram", [128, NC], PLANE),
 }
-SEMAPHORES = ["sent", "cA", "cPA", "cB", "cPB", "cC", "cPC", "lx", "mm", "vv", "aa", "xq", "gq", "hq", "hl"]
-for _j in range(G):
-    for _k in ("a", "b"):
+SEMAPHORES = ["sent", "lx", "mm", "vv", "aa"]
+for _k, _n in (("a", G), ("b", G), ("c", N)):
+    SEMAPHORES += ["od" + _k, "op" + _k]
+    for _j in range(_n):
         SCRATCH["d%s%d" % (_k, _j)] = ("dram", [128, NC], CODES)
         SCRATCH["p%s%d" % (_k, _j)] = ("dram", [128, NC], PLANE)
-        SEMAPHORES += ["d%s%d" % (_k, _j), "p%s%d" % (_k, _j)]
-    SEMAPHORES += ["lw%d" % _j]
-for _j in range(2):
-    SCRATCH["dh%d" % _j] = ("dram", [128, NC], CODES)
-    SCRATCH["ph%d" % _j] = ("dram", [128, NC], PLANE)
-    SEMAPHORES += ["dh%d" % _j, "ph%d" % _j]
-for _j in range(P):
-    SCRATCH["dc%d" % _j] = ("dram", [128, 2 * NC], CODES)
-    SCRATCH["pc%d" % _j] = ("dram", [128, 2 * NC], PLANE)
-    SEMAPHORES += ["dc%d" % _j, "pc%d" % _j, "lc%d" % _j, "st%d" % _j]
+        SEMAPHORES += ["d%s%d" % (_k, _j), "p%s%d" % (_k, _j), "l%s%d" % (_k, _j)]
+SEMAPHORES += ["st%d" % _j for _j in range(P)]
 
 
 def _bits(mask):
     return [1 << i for i in range(32) if mask >> i & 1]
 
 
+def _split(mask, parts):
+    b = _bits(mask)
+    n = len(b) // parts
+    return [sum(b[i * n:(i + 1) * n]) for i in range(parts)]
+
+
 def _helpers(T, topo):
     out = {}
     for p in range(P):
-        u = T.cores[2 * p]
-        for d in (topo.die(u), topo.die(T.cores[2 * p + 1])):
-            free = [c for c in range(SIM) if topo.chip(c) == topo.chip(u) and topo.die(c) == d and T.rank_of(c) is None]
-            out[free[0]] = (p, d)
+        for d in range(2):
+            u = T.cores[2 * p + d]
+            free = [c for c in range(SIM) if topo.chip(c) == topo.chip(u) and topo.die(c) == topo.die(u)
+                    and T.rank_of(c) is None]
+            out["recv", p, d] = free[0]
+            if 2 * p < G:
+                out["send", p, d] = free[1]
     return out
-
-
-def _waves(p):
-    held = G // 2
-    rest = list(range(held, P))
-    if p == 0:
-        return [1, rest[0]] + rest[1:]
-    return rest[1:] + [rest[0], 0]
 
 
 def _plan(T, topo, core):
     helpers = _helpers(T, topo)
+    role = {helpers[k]: k for k in helpers}.get(core)
     calls = []
-    if core in helpers:
-        p, d = helpers[core]
-        same = {helpers[h][0]: h for h in helpers if helpers[h][1] == d}
-        steps = (1, 2) if d == topo.die(T.cores[0]) else (3, 4)
-        away = [same[(p + k) % P] for k in steps]
+    if role is not None:
+        kind, p, d = role
         ranks = [T.cores[2 * p], T.cores[2 * p + 1]]
-        here = [c for c in ranks if topo.die(c) == d]
-        off = topo.mask(core, away[0])
-        every = topo.mask(core, here[0])
-        for k in "dp":
-            name = "%sc%d" % (k, p)
-            calls.append(([("hl", 64)] if k == "d" else [],
-                          [(name, name, name, off, away), (name, name, name, every & ~off, here)]))
-        for q in sorted(((p - k) % P for k in steps), key=lambda q: (2 * q < G, q)):
-            for k in "dp":
-                name = "%sc%d" % (k, q)
-                calls.append(([(name, None)], [(name, name, name, every, ranks)]))
+        rest = [s for s in range(P) if s != p]
+        if kind == "send":
+            j = 2 * p + d
+            off = topo.mask(core, T.cores[2 * rest[0] + d])
+            for k, dsts in (("b", [T.cores[2 * s + d] for s in rest]), ("c", [helpers["recv", s, d] for s in rest])):
+                for c in "dp":
+                    name = "%s%s%d" % (c, k, j)
+                    calls.append(([name], [(name, off, dsts)]))
+            return calls
+        every = topo.mask(core, ranks[0])
+        for part in ([s for s in rest if 2 * s >= G], [s for s in rest if 2 * s < G]):
+            for i in range(0, len(part), 2):
+                two = part[i:i + 2]
+                for c in "dp":
+                    names = ["%sc%d" % (c, 2 * s + d) for s in two]
+                    calls.append((names, [(n, m, ranks) for n, m in zip(names, _split(every, len(two)))]))
         return calls
     r = T.rank_of(core)
     if r is None:
         return calls
-    p, odd = divmod(r, 2)
+    p, d = divmod(r, 2)
     partner = T.cores[r ^ 1]
-    mine = [h for h in helpers if helpers[h][0] == p]
-    a_users = [T.cores[2 * s] for s in range(P) if s != p]
-    b_users = [T.cores[2 * s + 1] for s in range(P) if s != p]
-    off = topo.mask(core, a_users[0])
+    rest = [s for s in range(P) if s != p]
+    same = [T.cores[2 * s + d] for s in rest]
+    off = topo.mask(core, same[0])
     every = topo.mask(core, partner)
     on = every & ~off
-    b = _bits(on)
-    on1, on2 = sum(b[:len(b) // 2]), sum(b[len(b) // 2:])
-
-    def tile(k, mask, dsts):
-        name = "%s%d" % (k, r)
-        return (name, name, name, mask, dsts)
-
-    def send_x(mask):
-        calls.append(([("vv", 1)], [("q3c", "q1vc", "xq", mask, [partner])]))
-        calls.append(([], [("q3s", "q1vs", "xq", mask, [partner])]))
-
     if r < G:
-        order = _waves(p)
-        for w in (order[:2], order[2:]):
-            dsts = [T.cores[2 * s] for s in w]
-            calls.append(([("cA", 16)], [tile("da", off, dsts)]))
-            calls.append(([("cPA", 16)], [tile("pa", off, dsts)]))
-        if odd:
-            send_x(on)
-        calls.append(([("cB", 16), ("cC", 16)], [tile("db", off, b_users), tile("da" if odd else "db", on1, [partner]),
-                                                 ("sc", "dh%d" % odd, "dh%d" % odd, on2, mine)]))
-        calls.append(([("cPB", 16), ("cPC", 16)], [tile("pb", off, b_users), tile("pa" if odd else "pb", on1, [partner]),
-                                                   ("sp", "ph%d" % odd, "ph%d" % odd, on2, mine)]))
+        send = helpers["send", p, d]
+        m = _split(on, 2)
+        for c in "dp":
+            calls.append((["o%sa" % c], [("%sa%d" % (c, r), off, same)]))
+        for c in "dp":
+            calls.append((["o%sb" % c], [("%sb%d" % (c, r), m[0], [send]), ("%sa%d" % (c, r), m[1], [partner])]))
+        for c in "dp":
+            calls.append((["o%sc" % c], [("%sb%d" % (c, r), m[0], [partner]), ("%sc%d" % (c, r), m[1], [send, partner])]))
+        relay = on
     else:
-        if odd:
-            send_x(every)
-        calls.append(([("cC", 16)], [("sc", "dh%d" % odd, "dh%d" % odd, every, mine)]))
-        calls.append(([("cPC", 16)], [("sp", "ph%d" % odd, "ph%d" % odd, every, mine)]))
-    if odd:
-        calls.append(([("vv", 4)], [("q2uc", "q3c", "hq", every, [partner])]))
-        calls.append(([], [("q2us", "q3s", "hq", every, [partner])]))
-    else:
-        calls.append(([("vv", 7)], [("q2c", "q1c", "gq", every, [partner])]))
-        calls.append(([], [("q2s", "q1s", "gq", every, [partner])]))
+        for c in "dp":
+            name = "%sc%d" % (c, r)
+            calls.append((["o%sc" % c], [(name, off, [helpers["recv", s, d] for s in rest]), (name, on, [partner])]))
+        relay = every
+    for k in "ab":
+        tiles = [j for j in range(G) if j % 2 == d and j // 2 != p]
+        for c in "dp":
+            names = ["%s%s%d" % (c, k, j) for j in tiles]
+            calls.append((names, [(n, m, [partner]) for n, m in zip(names, _split(relay, len(tiles)))]))
     return calls
 
 
 def rank_program(g, core, T, topo):
     helpers = _helpers(T, topo)
     r = T.rank_of(core)
-    if r is None and core not in helpers:
+    if r is None and core not in helpers.values():
         return
 
-    arrive = {}
-    for c in list(T.cores) + list(helpers):
+    arrive = {"o%s%s" % (c, k): 16 for c in "dp" for k in "abc"}
+    for c in list(T.cores) + list(helpers.values()):
         if c != core:
             for _, transfers in _plan(T, topo, c):
-                for _, _, sem, mask, dsts in transfers:
+                for name, mask, dsts in transfers:
                     if core in dsts:
-                        arrive[sem] = arrive.get(sem, 0) + len(_bits(mask))
-
-    views = {"q1c": T.q1[:].bitcast(dt.uint8), "q1s": T.q1s[:],
-             "q1vc": T.q1[:, NC:2 * NC].bitcast(dt.uint8), "q1vs": T.q1s[:, NC:2 * NC],
-             "q2c": T.q2[:].bitcast(dt.uint8), "q2s": T.q2s[:],
-             "q2uc": T.q2[:, 0:NC].bitcast(dt.uint8), "q2us": T.q2s[:, 0:NC],
-             "q3c": T.q3[:].bitcast(dt.uint8), "q3s": T.q3s[:],
-             "sc": T.sc[:].bitcast(dt.uint8), "sp": T.sp[:]}
+                        arrive[name] = arrive.get(name, 0) + len(_bits(mask))
 
     def raw(name):
-        if name in views:
-            return views[name]
         return T[name][:].bitcast(dt.uint8) if name[0] == "d" else T[name][:]
 
     def remote():
         sent = 0
         for waits, transfers in _plan(T, topo, core):
-            for sem, count in waits:
-                g.wait_ge(T.sem[sem], arrive[sem] if count is None else count)
+            for sem in waits:
+                g.wait_ge(T.sem[sem], arrive[sem])
             out = []
-            for src, dst, sem, mask, dsts in transfers:
+            for name, mask, dsts in transfers:
                 ids = []
                 for d in dsts:
                     rid, pid, _ = topo.addr(d)
                     ids.append(DstId(rid=rid, pnc=pid))
-                out.append(RemoteDMATransfer(dst_ids=ids, dma_engine_mask=mask, remote_sem=T.sem[sem],
-                                             srcs=[raw(src)], dsts=[raw(dst) for _ in dsts]))
+                out.append(RemoteDMATransfer(dst_ids=ids, dma_engine_mask=mask, remote_sem=T.sem[name],
+                                             srcs=[raw(name)], dsts=[raw(name) for _ in dsts]))
                 sent += len(_bits(mask))
             g.remote_dma_fused(out, local_sem=T.sem.sent)
         g.wait_ge(T.sem.sent, sent)
 
     if r is None:
-        p = helpers[core][0]
-        for k in "dp":
-            for j in range(2):
-                name = "%sh%d" % (k, j)
-                half = T["%sc%d" % (k, p)][:, j * NC:(j + 1) * NC]
-                g.sync.wait_ge(T.sem[name], arrive[name])
-                g.sync.dma_start(half.bitcast(dt.uint8) if k == "d" else half, raw(name)).then_inc(T.sem.hl, 16)
         remote()
         return
 
     pair, odd = divmod(r, 2)
-    holds = r < G
-    lk = "b" if odd else "a"
-    own = {"da": T.ac, "pa": T.az, "db": T.bc, "pb": T.bs}
+    own = {"da": T.ac, "pa": T.az, "db": T.bc, "pb": T.bs, "dc": T.cc, "pc": T.cs}
 
-    if holds:
-        for k, sem in (("da", "cA"), ("pa", "cPA"), ("db", "cB"), ("pb", "cPB")):
-            g.scalar.dma_start(raw("%s%d" % (k, r)), own[k][:]).then_inc(T.sem[sem], 16)
-    g.scalar.dma_start(raw("sc"), T.cc[:]).then_inc(T.sem.cC, 16)
-    g.scalar.dma_start(raw("sp"), T.cs[:]).then_inc(T.sem.cPC, 16)
+    for k in ("abc" if r < G else "c"):
+        for c in "dp":
+            g.scalar.dma_start(raw("%s%s%d" % (c, k, r)), own[c + k][:]).then_inc(T.sem["o" + c + k], 16)
 
     remote()
 
+    ws = sorted(range(G), key=lambda s: (s != r, s // 2 != pair, s % 2 != odd, s))
     pairs = sorted(range(P), key=lambda p: (pair != p, 2 * p < G, p))
-    early = {s: pair in _waves(s)[:2] for s in range(G // 2) if s != pair}
-    ws = sorted(range(G), key=lambda s: (s != r, s // 2 != pair, not early.get(s // 2, False), s))
+    cs = []
+    for p in pairs:
+        cs += [r, r ^ 1] if p == pair else [2 * p, 2 * p + 1]
 
-    def slot(i):
-        a = (i % 2) * NC
-        return T.w[:, a:a + NC], T.ws[:, a:a + NC]
+    def slot(k, i):
+        a = (i % (WC if k == "c" else WA)) * NC
+        return T["w" + k][:, a:a + NC], T["w" + k + "s"][:, a:a + NC]
 
-    def load(i):
-        s = ws[i]
-        w, wp = slot(i)
-        if i >= 2:
-            g.sync.wait_ge(T.sem.mm, i - 1)
-        sem = T.sem["lw%d" % i]
+    first = {"a": 0, "b": G, "c": 2 * G}
+
+    def load(k, i):
+        j = (cs if k == "c" else ws)[i]
+        w, wp = slot(k, i)
+        back = i - (WC if k == "c" else WA)
+        if back >= 0:
+            g.sync.wait_ge(T.sem.mm, first[k] + back + 1)
         for c, view in (("d", w.bitcast(dt.uint8)), ("p", wp)):
-            name = "%s%s%d" % (c, lk, s)
-            if s == r:
-                g.sync.dma_start(view, own[c + lk][:]).then_inc(sem, 16)
+            name = "%s%s%d" % (c, k, j)
+            if j == r:
+                g.sync.dma_start(view, own[c + k][:]).then_inc(T.sem["l%s%d" % (k, i)], 16)
             else:
                 g.sync.wait_ge(T.sem[name], arrive[name])
-                g.sync.dma_start(view, raw(name)).then_inc(sem, 16)
+                g.sync.dma_start(view, raw(name)).then_inc(T.sem["l%s%d" % (k, i)], 16)
 
     g.sync.dma_start(T.tx[:], T.x[:]).then_inc(T.sem.lx, 16)
-    for i in range(G):
-        load(i)
-    for i in range(P):
-        if i:
-            g.sync.wait_ge(T.sem.mm, G + 2 * i)
-        for c, view in (("d", T.wc[:].bitcast(dt.uint8)), ("p", T.wcs[:])):
-            name = "%sc%d" % (c, pairs[i])
-            g.sync.wait_ge(T.sem[name], arrive[name])
-            g.sync.dma_start(view, raw(name)).then_inc(T.sem["lc%d" % i], 16)
+    if r < G:
+        order = [("a", 0), ("a", 1), ("b", 0), ("c", 0), ("a", 2), ("a", 3), ("b", 1), ("b", 2), ("b", 3)]
+    else:
+        order = [("c", 0), ("a", 0), ("a", 1), ("a", 2), ("a", 3), ("b", 0), ("b", 1), ("b", 2), ("b", 3)]
+    for k, i in order + [("c", i) for i in range(1, N)]:
+        load(k, i)
 
     def bank(n):
         return (n % 8) * 512
 
-    if odd:
-        g.tensor.wait_ge(T.sem.gq, arrive["gq"])
-    else:
-        g.tensor.wait_ge(T.sem.vv, 1)
-        g.tensor.wait_ge(T.sem.xq, arrive["xq"])
-    for i in range(G):
-        g.tensor.wait_ge(T.sem["lw%d" % i], 32)
-        w, wp = slot(i)
-        g.tensor.matmul_mx(T.ps[:, bank(i):bank(i) + 2 * NC], w, wp, T.q1[:], T.q1s[:], True, True).then_inc(T.sem.mm, 1)
-    g.tensor.wait_ge(T.sem.aa, 4)
+    for k, ready in (("a", 1), ("b", 4)):
+        q, qs = (T.qx, T.qxs) if k == "a" else (T.q2, T.q2s)
+        g.tensor.wait_ge(T.sem.vv, ready)
+        for i in range(G):
+            g.tensor.wait_ge(T.sem["l%s%d" % (k, i)], 32)
+            w, wp = slot(k, i)
+            n = bank(first[k] + i)
+            g.tensor.matmul_mx(T.ps[:, n:n + NC], w, wp, q[:], qs[:], True, True).then_inc(T.sem.mm, 1)
     g.tensor.wait_ge(T.sem.vv, 7)
-    if odd:
-        hq, hs = T.q2[:, NC:2 * NC], T.q2s[:, NC:2 * NC]
-    else:
-        g.tensor.wait_ge(T.sem.hq, arrive["hq"])
-        hq, hs = T.q3[:], T.q3s[:]
     for i in range(N):
-        n = G + i
         if i == 8:
             g.tensor.wait_ge(T.sem.vv, 8)
         if i == 9:
             g.tensor.wait_ge(T.sem.aa, 5)
-        if i % 2 == 0:
-            g.tensor.wait_ge(T.sem["lc%d" % (i // 2)], 32)
-        a = (i % 2) * NC
-        g.tensor.matmul_mx(T.ps[:, bank(n):bank(n) + NC], T.wc[:, a:a + NC], T.wcs[:, a:a + NC], hq, hs,
-                           True, True).then_inc(T.sem.mm, 1)
+        g.tensor.wait_ge(T.sem["lc%d" % i], 32)
+        w, wp = slot("c", i)
+        n = bank(i)
+        g.tensor.matmul_mx(T.ps[:, n:n + NC], w, wp, T.q2[:], T.q2s[:], True, True).then_inc(T.sem.mm, 1)
 
     g.vector.wait_ge(T.sem.lx, 16)
-    if odd:
-        g.vector.quantize_mx(T.q3[:], T.q3s[:], T.tx[:]).then_inc(T.sem.vv, 1)
-    else:
-        g.vector.quantize_mx(T.q1[:, 0:NC], T.q1s[:, 0:NC], T.tx[:]).then_inc(T.sem.vv, 1)
-    for half in range(2):
-        a = half * NC
-        if half:
-            g.vector.wait_ge(T.sem.vv, 4)
-        for i in (0, 2):
-            b = ws[i]
-            g.vector.wait_ge(T.sem.mm, i + 1)
-            g.vector.tensor_scalar(T.t2[:, b:4 * NC:4], T.ps[:, bank(i) + a:bank(i) + a + NC], 0.0, SCALE,
+    g.vector.quantize_mx(T.qx[:], T.qxs[:], T.tx[:]).then_inc(T.sem.vv, 1)
+    for h, k in enumerate("ab"):
+        for i in (1, 3):
+            n = bank(first[k] + i)
+            g.vector.wait_ge(T.sem.mm, first[k] + i + 1)
+            g.vector.tensor_scalar(T.t2[:, ws[i]:4 * NC:4], T.ps[:, n:n + NC], 0.0, SCALE,
                                    AluOpType.max, AluOpType.mult).then_inc(T.sem.vv, 1)
-        g.vector.wait_ge(T.sem.vv, 3 + 3 * half)
-        g.vector.wait_ge(T.sem.aa, 2 + 2 * half)
-        g.vector.quantize_mx(T.q2[:, a:a + NC], T.q2s[:, a:a + NC], T.t2[:]).then_inc(T.sem.vv, 1)
+        g.vector.wait_ge(T.sem.aa, 2 + 2 * h)
+        g.vector.wait_ge(T.sem.vv, 3 + 3 * h)
+        g.vector.quantize_mx(T.q2[:], T.q2s[:], T.t2[:]).then_inc(T.sem.vv, 1)
     for p in range(P):
-        n = G + 2 * p
+        i = 2 * p
+        a = (cs[i] % 2) * NC
         if p >= 1:
             g.vector.wait_ge(T.sem["st%d" % (p - 1)], 16)
-        g.vector.wait_ge(T.sem.mm, n + 1)
-        g.vector.tensor_copy(T.stage[:, 0:NC], T.ps[:, bank(n):bank(n) + NC]).then_inc(T.sem.vv, 1)
+        g.vector.wait_ge(T.sem.mm, 2 * G + i + 1)
+        g.vector.tensor_copy(T.stage[:, a:a + NC], T.ps[:, bank(i):bank(i) + NC]).then_inc(T.sem.vv, 1)
 
-    for half in range(2):
-        a = half * NC
-        if half:
-            g.scalar.wait_ge(T.sem.vv, 4)
-        for i in (1, 3):
-            b = ws[i]
-            g.scalar.wait_ge(T.sem.mm, i + 1)
-            g.scalar.activation(T.t2[:, b:4 * NC:4], T.ps[:, bank(i) + a:bank(i) + a + NC],
+    for k in "ab":
+        for i in (0, 2):
+            n = bank(first[k] + i)
+            g.scalar.wait_ge(T.sem.mm, first[k] + i + 1)
+            g.scalar.activation(T.t2[:, ws[i]:4 * NC:4], T.ps[:, n:n + NC],
                                 ActivationFunctionType.Relu, scale=SCALE).then_inc(T.sem.aa, 1)
     for p in range(P):
-        n = G + 2 * p + 1
+        i = 2 * p + 1
+        a = (cs[i] % 2) * NC
         if p >= 1:
             g.scalar.wait_ge(T.sem["st%d" % (p - 1)], 16)
-        g.scalar.wait_ge(T.sem.mm, n + 1)
-        g.scalar.activation(T.stage[:, NC:2 * NC], T.ps[:, bank(n):bank(n) + NC], ActivationFunctionType.Copy).then_inc(T.sem.aa, 1)
+        g.scalar.wait_ge(T.sem.mm, 2 * G + i + 1)
+        g.scalar.activation(T.stage[:, a:a + NC], T.ps[:, bank(i):bank(i) + NC], ActivationFunctionType.Copy).then_inc(T.sem.aa, 1)
         g.scalar.wait_ge(T.sem.vv, 8 + p)
         g.scalar.wait_ge(T.sem.aa, 5 + p)
         y = pairs[p] * 2 * NC

@@ -33,7 +33,7 @@ for _k, _n in (("a", G), ("b", G), ("c", N)):
         SCRATCH["d%s%d" % (_k, _j)] = ("dram", [128, NC], CODES)
         SCRATCH["p%s%d" % (_k, _j)] = ("dram", [128, NC], PLANE)
         SEMAPHORES += ["d%s%d" % (_k, _j), "p%s%d" % (_k, _j), "l%s%d" % (_k, _j)]
-SEMAPHORES += ["st%d" % _j for _j in range(P)]
+SEMAPHORES += ["st%d" % _j for _j in range(N)]
 
 
 def _bits(mask):
@@ -62,20 +62,27 @@ def _helpers(T, topo):
 def _plan(T, topo, core):
     helpers = _helpers(T, topo)
     role = {helpers[k]: k for k in helpers}.get(core)
+    r = T.rank_of(core)
     calls = []
+    if role is None and r is None:
+        return calls
+    p, d = divmod(r, 2) if role is None else role[1:]
+    rest = sorted((s for s in range(P) if s != p), key=lambda s: (2 * s < G, s if p % 2 == 0 else -s))
+    ranks = [T.cores[2 * p], T.cores[2 * p + 1]]
+    same = [T.cores[2 * s + d] for s in rest]
+    recv = [helpers["recv", s, d] for s in rest]
+    partner = ranks[1 - d]
+    off = topo.mask(core, same[0])
+    every = topo.mask(core, partner)
+    on = every & ~off
+
+    if role is not None and role[0] == "send":
+        for k, dsts in (("b", same), ("c", recv)):
+            for c in "dp":
+                name = "%s%s%d" % (c, k, 2 * p + d)
+                calls.append(([name], [(name, off, dsts), (name, on, [partner])]))
+        return calls
     if role is not None:
-        kind, p, d = role
-        ranks = [T.cores[2 * p], T.cores[2 * p + 1]]
-        rest = [s for s in range(P) if s != p]
-        if kind == "send":
-            j = 2 * p + d
-            off = topo.mask(core, T.cores[2 * rest[0] + d])
-            for k, dsts in (("b", [T.cores[2 * s + d] for s in rest]), ("c", [helpers["recv", s, d] for s in rest])):
-                for c in "dp":
-                    name = "%s%s%d" % (c, k, j)
-                    calls.append(([name], [(name, off, dsts)]))
-            return calls
-        every = topo.mask(core, ranks[0])
         for part in ([s for s in rest if 2 * s >= G], [s for s in rest if 2 * s < G]):
             for i in range(0, len(part), 2):
                 two = part[i:i + 2]
@@ -83,16 +90,13 @@ def _plan(T, topo, core):
                     names = ["%sc%d" % (c, 2 * s + d) for s in two]
                     calls.append((names, [(n, m, ranks) for n, m in zip(names, _split(every, len(two)))]))
         return calls
-    r = T.rank_of(core)
-    if r is None:
-        return calls
-    p, d = divmod(r, 2)
-    partner = T.cores[r ^ 1]
-    rest = [s for s in range(P) if s != p]
-    same = [T.cores[2 * s + d] for s in rest]
-    off = topo.mask(core, same[0])
-    every = topo.mask(core, partner)
-    on = every & ~off
+
+    def passed(k, mask):
+        tiles = [j for j in range(G) if j % 2 == d and j // 2 != p]
+        for c in "dp":
+            names = ["%s%s%d" % (c, k, j) for j in tiles]
+            calls.append((names, [(n, m, [partner]) for n, m in zip(names, _split(mask, len(tiles)))]))
+
     if r < G:
         send = helpers["send", p, d]
         m = _split(on, 2)
@@ -100,19 +104,16 @@ def _plan(T, topo, core):
             calls.append((["o%sa" % c], [("%sa%d" % (c, r), off, same)]))
         for c in "dp":
             calls.append((["o%sb" % c], [("%sb%d" % (c, r), m[0], [send]), ("%sa%d" % (c, r), m[1], [partner])]))
+        passed("a", on)
         for c in "dp":
-            calls.append((["o%sc" % c], [("%sb%d" % (c, r), m[0], [partner]), ("%sc%d" % (c, r), m[1], [send, partner])]))
-        relay = on
+            calls.append((["o%sc" % c], [("%sc%d" % (c, r), on, [send])]))
+        passed("b", on)
     else:
         for c in "dp":
             name = "%sc%d" % (c, r)
-            calls.append((["o%sc" % c], [(name, off, [helpers["recv", s, d] for s in rest]), (name, on, [partner])]))
-        relay = every
-    for k in "ab":
-        tiles = [j for j in range(G) if j % 2 == d and j // 2 != p]
-        for c in "dp":
-            names = ["%s%s%d" % (c, k, j) for j in tiles]
-            calls.append((names, [(n, m, [partner]) for n, m in zip(names, _split(relay, len(tiles)))]))
+            calls.append((["o%sc" % c], [(name, off, recv), (name, on, [partner])]))
+        passed("a", every)
+        passed("b", every)
     return calls
 
 
@@ -133,6 +134,17 @@ def rank_program(g, core, T, topo):
     def raw(name):
         return T[name][:].bitcast(dt.uint8) if name[0] == "d" else T[name][:]
 
+    def slot(k, i):
+        a = (i % (WC if k == "c" else WA)) * NC
+        return T["w" + k][:, a:a + NC], T["w" + k + "s"][:, a:a + NC]
+
+    def landing(name, dst):
+        q = T.rank_of(dst)
+        if q is None or int(name[2:]) != q ^ 1:
+            return raw(name)
+        w, wp = slot(name[1], 1)
+        return w.bitcast(dt.uint8) if name[0] == "d" else wp
+
     def remote():
         sent = 0
         for waits, transfers in _plan(T, topo, core):
@@ -145,7 +157,7 @@ def rank_program(g, core, T, topo):
                     rid, pid, _ = topo.addr(d)
                     ids.append(DstId(rid=rid, pnc=pid))
                 out.append(RemoteDMATransfer(dst_ids=ids, dma_engine_mask=mask, remote_sem=T.sem[name],
-                                             srcs=[raw(name)], dsts=[raw(name) for _ in dsts]))
+                                             srcs=[raw(name)], dsts=[landing(name, d) for d in dsts]))
                 sent += len(_bits(mask))
             g.remote_dma_fused(out, local_sem=T.sem.sent)
         g.wait_ge(T.sem.sent, sent)
@@ -163,15 +175,11 @@ def rank_program(g, core, T, topo):
 
     remote()
 
-    ws = sorted(range(G), key=lambda s: (s != r, s // 2 != pair, s % 2 != odd, s))
+    ws = sorted(range(G), key=lambda s: (s != r, s // 2 != pair, s % 2 != odd, s if pair <= P // 2 else -s))
     pairs = sorted(range(P), key=lambda p: (pair != p, 2 * p < G, p))
     cs = []
     for p in pairs:
         cs += [r, r ^ 1] if p == pair else [2 * p, 2 * p + 1]
-
-    def slot(k, i):
-        a = (i % (WC if k == "c" else WA)) * NC
-        return T["w" + k][:, a:a + NC], T["w" + k + "s"][:, a:a + NC]
 
     first = {"a": 0, "b": G, "c": 2 * G}
 
@@ -189,13 +197,38 @@ def rank_program(g, core, T, topo):
                 g.sync.wait_ge(T.sem[name], arrive[name])
                 g.sync.dma_start(view, raw(name)).then_inc(T.sem["l%s%d" % (k, i)], 16)
 
+    def loaded(k, i):
+        j = (cs if k == "c" else ws)[i]
+        if j == r ^ 1:
+            for c in "dp":
+                name = "%s%s%d" % (c, k, j)
+                g.tensor.wait_ge(T.sem[name], arrive[name])
+        else:
+            g.tensor.wait_ge(T.sem["l%s%d" % (k, i)], 32)
+
+    def stage(i):
+        return T.stage[:, i % 2 * NC:(i % 2 + 1) * NC]
+
+    def store(queue, i):
+        y = cs[i] * NC
+        queue.dma_start(T.y[:, y:y + NC], stage(i)).then_inc(T.sem["st%d" % i], 16)
+
     g.sync.dma_start(T.tx[:], T.x[:]).then_inc(T.sem.lx, 16)
     if r < G:
-        order = [("a", 0), ("a", 1), ("b", 0), ("c", 0), ("a", 2), ("a", 3), ("b", 1), ("b", 2), ("b", 3)]
+        order = "a0 a2 b0 a3 c0 b2 b3 c2"
     else:
-        order = [("c", 0), ("a", 0), ("a", 1), ("a", 2), ("a", 3), ("b", 0), ("b", 1), ("b", 2), ("b", 3)]
-    for k, i in order + [("c", i) for i in range(1, N)]:
-        load(k, i)
+        order = "c0 a0 a1 a2 a3 b0 b1 b2 b3 c2"
+    for s in order.split():
+        load(s[0], int(s[1]))
+    for i in range(0, N, 2):
+        if i + WC < N:
+            load("c", i + WC)
+        g.sync.wait_ge(T.sem.vv, 8 + i // 2)
+        store(g.sync, i)
+        if i + WC + 1 < N:
+            g.sync.wait_ge(T.sem.aa, 5 + i // 2)
+            load("c", i + WC + 1)
+    g.sync.wait_ge(T.sem["st%d" % (N - 2)], 16)
 
     def bank(n):
         return (n % 8) * 512
@@ -204,7 +237,7 @@ def rank_program(g, core, T, topo):
         q, qs = (T.qx, T.qxs) if k == "a" else (T.q2, T.q2s)
         g.tensor.wait_ge(T.sem.vv, ready)
         for i in range(G):
-            g.tensor.wait_ge(T.sem["l%s%d" % (k, i)], 32)
+            loaded(k, i)
             w, wp = slot(k, i)
             n = bank(first[k] + i)
             g.tensor.matmul_mx(T.ps[:, n:n + NC], w, wp, q[:], qs[:], True, True).then_inc(T.sem.mm, 1)
@@ -214,7 +247,7 @@ def rank_program(g, core, T, topo):
             g.tensor.wait_ge(T.sem.vv, 8)
         if i == 9:
             g.tensor.wait_ge(T.sem.aa, 5)
-        g.tensor.wait_ge(T.sem["lc%d" % i], 32)
+        loaded("c", i)
         w, wp = slot("c", i)
         n = bank(i)
         g.tensor.matmul_mx(T.ps[:, n:n + NC], w, wp, T.q2[:], T.q2s[:], True, True).then_inc(T.sem.mm, 1)
@@ -230,13 +263,11 @@ def rank_program(g, core, T, topo):
         g.vector.wait_ge(T.sem.aa, 2 + 2 * h)
         g.vector.wait_ge(T.sem.vv, 3 + 3 * h)
         g.vector.quantize_mx(T.q2[:], T.q2s[:], T.t2[:]).then_inc(T.sem.vv, 1)
-    for p in range(P):
-        i = 2 * p
-        a = (cs[i] % 2) * NC
-        if p >= 1:
-            g.vector.wait_ge(T.sem["st%d" % (p - 1)], 16)
+    for i in range(0, N, 2):
+        if i >= 2:
+            g.vector.wait_ge(T.sem["st%d" % (i - 2)], 16)
         g.vector.wait_ge(T.sem.mm, 2 * G + i + 1)
-        g.vector.tensor_copy(T.stage[:, a:a + NC], T.ps[:, bank(i):bank(i) + NC]).then_inc(T.sem.vv, 1)
+        g.vector.tensor_copy(stage(i), T.ps[:, bank(i):bank(i) + NC]).then_inc(T.sem.vv, 1)
 
     for k in "ab":
         for i in (0, 2):
@@ -244,15 +275,11 @@ def rank_program(g, core, T, topo):
             g.scalar.wait_ge(T.sem.mm, first[k] + i + 1)
             g.scalar.activation(T.t2[:, ws[i]:4 * NC:4], T.ps[:, n:n + NC],
                                 ActivationFunctionType.Relu, scale=SCALE).then_inc(T.sem.aa, 1)
-    for p in range(P):
-        i = 2 * p + 1
-        a = (cs[i] % 2) * NC
-        if p >= 1:
-            g.scalar.wait_ge(T.sem["st%d" % (p - 1)], 16)
+    for i in range(1, N, 2):
+        if i >= 3:
+            g.scalar.wait_ge(T.sem["st%d" % (i - 2)], 16)
         g.scalar.wait_ge(T.sem.mm, 2 * G + i + 1)
-        g.scalar.activation(T.stage[:, a:a + NC], T.ps[:, bank(i):bank(i) + NC], ActivationFunctionType.Copy).then_inc(T.sem.aa, 1)
-        g.scalar.wait_ge(T.sem.vv, 8 + p)
-        g.scalar.wait_ge(T.sem.aa, 5 + p)
-        y = pairs[p] * 2 * NC
-        g.scalar.dma_start(T.y[:, y:y + 2 * NC], T.stage[:]).then_inc(T.sem["st%d" % p], 16)
-    g.scalar.wait_ge(T.sem["st%d" % (P - 1)], 16)
+        g.scalar.activation(stage(i), T.ps[:, bank(i):bank(i) + NC], ActivationFunctionType.Copy).then_inc(T.sem.aa, 1)
+        g.scalar.wait_ge(T.sem.aa, 5 + i // 2)
+        store(g.scalar, i)
+    g.scalar.wait_ge(T.sem["st%d" % (N - 1)], 16)

from concourse.bass import DstId, RemoteDMATransfer
from concourse.mybir import dt, AluOpType, ActivationFunctionType

N = 10
P = N // 2
G = 4
NC = 128
SIM = 80
SCALE = 0.037
WA, WC = 2, 3

CODES, PLANE = "float8_e4m3fn_x4", "uint8"
SCRATCH = {
    "tx": ("sbuf", [128, 4 * NC], "bfloat16"),
    "t2": ("sbuf", [128, 4 * NC], "bfloat16"),
    "qx": ("sbuf", [128, NC], CODES),
    "qxs": ("sbuf", [128, NC], PLANE),
    "q2": ("sbuf", [128, NC], CODES),
    "q2s": ("sbuf", [128, NC], PLANE),
    "wa": ("sbuf", [128, WA * NC], CODES),
    "was": ("sbuf", [128, WA * NC], PLANE),
    "wb": ("sbuf", [128, WA * NC], CODES),
    "wbs": ("sbuf", [128, WA * NC], PLANE),
    "wc": ("sbuf", [128, WC * NC], CODES),
    "wcs": ("sbuf", [128, WC * NC], PLANE),
    "stage": ("sbuf", [128, 2 * NC], "float32"),
    "ps": ("psum", [128, 4096], "float32"),
}
SEMAPHORES = ["sent", "lx", "mm", "vv", "aa"]
for _k, _n in (("a", G), ("b", G), ("c", N)):
    SEMAPHORES += ["od" + _k, "op" + _k]
    for _j in range(_n):
        SCRATCH["d%s%d" % (_k, _j)] = ("dram", [128, NC], CODES)
        SCRATCH["p%s%d" % (_k, _j)] = ("dram", [128, NC], PLANE)
        SEMAPHORES += ["d%s%d" % (_k, _j), "p%s%d" % (_k, _j), "l%s%d" % (_k, _j)]
SEMAPHORES += ["st%d" % _j for _j in range(N)]


def _bits(mask):
    return [1 << i for i in range(32) if mask >> i & 1]


def _split(mask, parts):
    b = _bits(mask)
    n = len(b) // parts
    return [sum(b[i * n:(i + 1) * n]) for i in range(parts)]


def _helpers(T, topo):
    out = {}
    for p in range(P):
        for d in range(2):
            u = T.cores[2 * p + d]
            free = [c for c in range(SIM) if topo.chip(c) == topo.chip(u) and topo.die(c) == topo.die(u)
                    and T.rank_of(c) is None]
            out["recv", p, d] = free[0]
            if 2 * p < G:
                out["send", p, d] = free[1]
    return out


def _plan(T, topo, core):
    helpers = _helpers(T, topo)
    role = {helpers[k]: k for k in helpers}.get(core)
    r = T.rank_of(core)
    calls = []
    if role is None and r is None:
        return calls
    p, d = divmod(r, 2) if role is None else role[1:]
    rest = sorted((s for s in range(P) if s != p), key=lambda s: (2 * s < G, s if p % 2 == 0 else -s))
    ranks = [T.cores[2 * p], T.cores[2 * p + 1]]
    same = [T.cores[2 * s + d] for s in rest]
    recv = [helpers["recv", s, d] for s in rest]
    partner = ranks[1 - d]
    off = topo.mask(core, same[0])
    every = topo.mask(core, partner)
    on = every & ~off

    if role is not None and role[0] == "send":
        for k, dsts in (("b", same), ("c", recv)):
            for c in "dp":
                name = "%s%s%d" % (c, k, 2 * p + d)
                calls.append(([name], [(name, off, dsts), (name, on, [partner])]))
        return calls
    if role is not None:
        for part in ([s for s in rest if 2 * s >= G], [s for s in rest if 2 * s < G]):
            for i in range(0, len(part), 2):
                two = part[i:i + 2]
                for c in "dp":
                    names = ["%sc%d" % (c, 2 * s + d) for s in two]
                    calls.append((names, [(n, m, ranks) for n, m in zip(names, _split(every, len(two)))]))
        return calls

    def passed(k, mask):
        tiles = [j for j in range(G) if j % 2 == d and j // 2 != p]
        for c in "dp":
            names = ["%s%s%d" % (c, k, j) for j in tiles]
            calls.append((names, [(n, m, [partner]) for n, m in zip(names, _split(mask, len(tiles)))]))

    if r < G:
        send = helpers["send", p, d]
        m = _split(on, 2)
        for c in "dp":
            calls.append((["o%sa" % c], [("%sa%d" % (c, r), off, same)]))
        for c in "dp":
            calls.append((["o%sb" % c], [("%sb%d" % (c, r), m[0], [send]), ("%sa%d" % (c, r), m[1], [partner])]))
        passed("a", on)
        for c in "dp":
            calls.append((["o%sc" % c], [("%sc%d" % (c, r), on, [send])]))
        passed("b", on)
    else:
        for c in "dp":
            name = "%sc%d" % (c, r)
            calls.append((["o%sc" % c], [(name, off, recv), (name, on, [partner])]))
        passed("a", every)
        passed("b", every)
    return calls


def rank_program(g, core, T, topo):
    helpers = _helpers(T, topo)
    r = T.rank_of(core)
    if r is None and core not in helpers.values():
        return

    arrive = {"o%s%s" % (c, k): 16 for c in "dp" for k in "abc"}
    for c in list(T.cores) + list(helpers.values()):
        if c != core:
            for _, transfers in _plan(T, topo, c):
                for name, mask, dsts in transfers:
                    if core in dsts:
                        arrive[name] = arrive.get(name, 0) + len(_bits(mask))

    def raw(name):
        return T[name][:].bitcast(dt.uint8) if name[0] == "d" else T[name][:]

    def slot(k, i):
        a = (i % (WC if k == "c" else WA)) * NC
        return T["w" + k][:, a:a + NC], T["w" + k + "s"][:, a:a + NC]

    def landing(name, dst):
        q = T.rank_of(dst)
        if q is None or int(name[2:]) != q ^ 1:
            return raw(name)
        w, wp = slot(name[1], 1)
        return w.bitcast(dt.uint8) if name[0] == "d" else wp

    def remote():
        sent = 0
        for waits, transfers in _plan(T, topo, core):
            for sem in waits:
                g.wait_ge(T.sem[sem], arrive[sem])
            out = []
            for name, mask, dsts in transfers:
                ids = []
                for d in dsts:
                    rid, pid, _ = topo.addr(d)
                    ids.append(DstId(rid=rid, pnc=pid))
                out.append(RemoteDMATransfer(dst_ids=ids, dma_engine_mask=mask, remote_sem=T.sem[name],
                                             srcs=[raw(name)], dsts=[landing(name, d) for d in dsts]))
                sent += len(_bits(mask))
            g.remote_dma_fused(out, local_sem=T.sem.sent)
        g.wait_ge(T.sem.sent, sent)

    if r is None:
        remote()
        return

    pair, odd = divmod(r, 2)
    own = {"da": T.ac, "pa": T.az, "db": T.bc, "pb": T.bs, "dc": T.cc, "pc": T.cs}

    for k in ("abc" if r < G else "c"):
        for c in "dp":
            g.scalar.dma_start(raw("%s%s%d" % (c, k, r)), own[c + k][:]).then_inc(T.sem["o" + c + k], 16)

    remote()

    ws = sorted(range(G), key=lambda s: (s != r, s // 2 != pair, s % 2 != odd, s if pair <= P // 2 else -s))
    pairs = sorted(range(P), key=lambda p: (pair != p, 2 * p < G, p))
    cs = []
    for p in pairs:
        cs += [r, r ^ 1] if p == pair else [2 * p, 2 * p + 1]

    first = {"a": 0, "b": G, "c": 2 * G}

    def load(k, i):
        j = (cs if k == "c" else ws)[i]
        w, wp = slot(k, i)
        back = i - (WC if k == "c" else WA)
        if back >= 0:
            g.sync.wait_ge(T.sem.mm, first[k] + back + 1)
        for c, view in (("d", w.bitcast(dt.uint8)), ("p", wp)):
            name = "%s%s%d" % (c, k, j)
            if j == r:
                g.sync.dma_start(view, own[c + k][:]).then_inc(T.sem["l%s%d" % (k, i)], 16)
            else:
                g.sync.wait_ge(T.sem[name], arrive[name])
                g.sync.dma_start(view, raw(name)).then_inc(T.sem["l%s%d" % (k, i)], 16)

    def loaded(k, i):
        j = (cs if k == "c" else ws)[i]
        if j == r ^ 1:
            for c in "dp":
                name = "%s%s%d" % (c, k, j)
                g.tensor.wait_ge(T.sem[name], arrive[name])
        else:
            g.tensor.wait_ge(T.sem["l%s%d" % (k, i)], 32)

    def stage(i):
        return T.stage[:, i % 2 * NC:(i % 2 + 1) * NC]

    def store(queue, i):
        y = cs[i] * NC
        queue.dma_start(T.y[:, y:y + NC], stage(i)).then_inc(T.sem["st%d" % i], 16)

    g.sync.dma_start(T.tx[:], T.x[:]).then_inc(T.sem.lx, 16)
    if r < G:
        order = "a0 a2 b0 a3 c0 b2 b3 c2"
    else:
        order = "c0 a0 a1 a2 a3 b0 b1 b2 b3 c2"
    for s in order.split():
        load(s[0], int(s[1]))
    for i in range(0, N, 2):
        if i + WC < N:
            load("c", i + WC)
        g.sync.wait_ge(T.sem.vv, 8 + i // 2)
        store(g.sync, i)
        if i + WC + 1 < N:
            g.sync.wait_ge(T.sem.aa, 5 + i // 2)
            load("c", i + WC + 1)
    g.sync.wait_ge(T.sem["st%d" % (N - 2)], 16)

    def bank(n):
        return (n % 8) * 512

    for k, ready in (("a", 1), ("b", 4)):
        q, qs = (T.qx, T.qxs) if k == "a" else (T.q2, T.q2s)
        g.tensor.wait_ge(T.sem.vv, ready)
        for i in range(G):
            loaded(k, i)
            w, wp = slot(k, i)
            n = bank(first[k] + i)
            g.tensor.matmul_mx(T.ps[:, n:n + NC], w, wp, q[:], qs[:], True, True).then_inc(T.sem.mm, 1)
    g.tensor.wait_ge(T.sem.vv, 7)
    for i in range(N):
        if i == 8:
            g.tensor.wait_ge(T.sem.vv, 8)
        if i == 9:
            g.tensor.wait_ge(T.sem.aa, 5)
        loaded("c", i)
        w, wp = slot("c", i)
        n = bank(i)
        g.tensor.matmul_mx(T.ps[:, n:n + NC], w, wp, T.q2[:], T.q2s[:], True, True).then_inc(T.sem.mm, 1)

    g.vector.wait_ge(T.sem.lx, 16)
    g.vector.quantize_mx(T.qx[:], T.qxs[:], T.tx[:]).then_inc(T.sem.vv, 1)
    for h, k in enumerate("ab"):
        for i in (1, 3):
            n = bank(first[k] + i)
            g.vector.wait_ge(T.sem.mm, first[k] + i + 1)
            g.vector.tensor_scalar(T.t2[:, ws[i]:4 * NC:4], T.ps[:, n:n + NC], 0.0, SCALE,
                                   AluOpType.max, AluOpType.mult).then_inc(T.sem.vv, 1)
        g.vector.wait_ge(T.sem.aa, 2 + 2 * h)
        g.vector.wait_ge(T.sem.vv, 3 + 3 * h)
        g.vector.quantize_mx(T.q2[:], T.q2s[:], T.t2[:]).then_inc(T.sem.vv, 1)
    for i in range(0, N, 2):
        if i >= 2:
            g.vector.wait_ge(T.sem["st%d" % (i - 2)], 16)
        g.vector.wait_ge(T.sem.mm, 2 * G + i + 1)
        g.vector.tensor_copy(stage(i), T.ps[:, bank(i):bank(i) + NC]).then_inc(T.sem.vv, 1)

    for k in "ab":
        for i in (0, 2):
            n = bank(first[k] + i)
            g.scalar.wait_ge(T.sem.mm, first[k] + i + 1)
            g.scalar.activation(T.t2[:, ws[i]:4 * NC:4], T.ps[:, n:n + NC],
                                ActivationFunctionType.Relu, scale=SCALE).then_inc(T.sem.aa, 1)
    for i in range(1, N, 2):
        if i >= 3:
            g.scalar.wait_ge(T.sem["st%d" % (i - 2)], 16)
        g.scalar.wait_ge(T.sem.mm, 2 * G + i + 1)
        g.scalar.activation(stage(i), T.ps[:, bank(i):bank(i) + NC], ActivationFunctionType.Copy).then_inc(T.sem.aa, 1)
        g.scalar.wait_ge(T.sem.aa, 5 + i // 2)
        store(g.scalar, i)
    g.scalar.wait_ge(T.sem["st%d" % (N - 1)], 16)
